import numpy as np
import ml_dtypes


def mxq(x, axis, fmt="e4m3"):
    dtype, down = {"e4m3": (ml_dtypes.float8_e4m3fn, 7), "e5m2": (ml_dtypes.float8_e5m2, 14)}[fmt]
    v = np.moveaxis(np.asarray(x, np.float32).astype(ml_dtypes.bfloat16).astype(np.float64), axis, -1)
    blocks = v.reshape(v.shape[:-1] + (-1, 32))
    amax = np.abs(blocks).max(-1, keepdims=True)
    byte = np.maximum(np.where(amax > 0, np.frexp(amax)[1] - 1 + 127, 0) - down, 1)
    scale = np.exp2(byte - 127.0)
    codes = (blocks / scale).astype(np.float32).astype(dtype).astype(np.float64)
    return np.moveaxis((codes * scale).reshape(v.shape), -1, axis)


WIDE = False


def mx_kscale(k):
    if not WIDE:
        return np.ones(k)
    levels = np.array([10, -10, 5, -5, 0])
    if k % 512:
        return np.exp2(np.random.permutation(np.resize(levels, k // 32))).repeat(32)
    a = np.empty((k // 512, 16))
    for p in range(k // 512):
        a[p, :8] = np.random.permutation(np.resize(levels, 8))
        for g in range(8):
            far = levels[np.abs(levels - a[p, g]) >= 10]
            a[p, g + 8] = far[np.random.randint(len(far))]
    return np.exp2(a.ravel()).repeat(32)


def f64(x):
    return np.asarray(x).astype(np.float64)


def striped(idx):
    return np.tile(idx.reshape(-1, 16).T, (8, 1)).astype(np.uint16)


def unstriped(offs):
    return offs[:16].T.reshape(-1).astype(np.int64)


def pack_weight(w):
    k, n = w.shape
    w = f64(np.asarray(w, np.float32).astype(ml_dtypes.bfloat16)).reshape(k // 32, 32, n)
    amax = np.abs(w).max(1)
    byte = np.clip(np.where(amax > 0, np.frexp(amax)[1] - 1 + 127 - 7, 1), 1, 254)
    scaled = (w * np.exp2(127.0 - byte)[:, None, :]).reshape(k, n).astype(np.float32)
    words = np.ascontiguousarray(scaled.reshape(k // 512, 128, 4, n).transpose(0, 1, 3, 2)).astype(ml_dtypes.float8_e4m3fn).view(np.uint8)
    return words, np.ascontiguousarray(byte.astype(np.uint8).reshape(k // 512, 16, n))


def unpack_weight(words, scales):
    g, p, n, _ = words.shape
    vals = np.ascontiguousarray(words).view(ml_dtypes.float8_e4m3fn).astype(np.float64) * np.repeat(np.exp2(scales.astype(np.float64) - 127.0), 8, axis=1)[..., None]
    return vals.transpose(0, 1, 3, 2).reshape(g * 512, n)


K, T, S, N, U = 1024, 1024, 512, 128, 1024
P = 2 ** 7


def setup_inputs():
    n = np.random.standard_normal
    s = mx_kscale(K)[:, None]
    packed_xT = pack_weight(n((K, T)) * s)
    return {
        "x_words": packed_xT[0],
        "x_scales": packed_xT[1],
        "w1": (n((K, N)) / np.sqrt(K) / s).astype(np.float32),
        "w2": (n((K, N)) / np.sqrt(K) / s).astype(np.float32),
        "cmap": (n((N, U)) * 0.7).astype(np.float32),
        "cap": (np.tile(np.random.uniform(0.4, 1.2, S), (P, 1))).astype(np.float32),
        "rate": (np.random.uniform(0.1, 0.6, (N, 1))).astype(np.float32),
        "offs": striped(np.random.permutation(T)[:S]),
        "cell": striped(np.random.permutation(U)[:S]),
    }


def reference(x_words, x_scales, w1, w2, cmap, cap, rate, offs, cell):
    m0 = f64(cmap)[:, unstriped(cell)]
    xq = unpack_weight(x_words, x_scales)[:, unstriped(offs)]
    z = np.log(((mxq(f64(w1), 0, "e4m3").T @ xq)) ** 2 + ((mxq(f64(w2), 0, "e4m3").T @ xq)) ** 2 + 0.1)
    df = z - m0
    nw = m0 + f64(rate) * (np.minimum(df, f64(cap)[:1]))
    out = f64(cmap).copy()
    out[:, unstriped(cell)] = nw
    return out

@@ -1,0 +1,153 @@
+from contextlib import ExitStack
+
+import concourse.mybir as mybir
+from concourse.masks import make_identity
+
+F32 = mybir.dt.float32
+BF16 = mybir.dt.bfloat16
+I32 = mybir.dt.int32
+U32 = mybir.dt.uint32
+U16 = mybir.dt.uint16
+U8 = mybir.dt.uint8
+FP8X4 = mybir.dt.float8_e4m3fn_x4
+ACT = mybir.ActivationFunctionType
+ALU = mybir.AluOpType
+
+P = 128
+K, T, S, N, U = 1024, 1024, 512, 128, 1024
+PASSES = 2
+CH = 128
+NCH = S // CH
+FLOPS = 2 * 2 * K * N * S
+
+
+def tile_picked_yclut_put_p_kernel(
+    tc, x_words, x_scales, w1, w2, cmap, cap, rate, offs, cell, out
+):
+    nc = tc.nc
+    with ExitStack() as ctx:
+        sb = ctx.enter_context(tc.tile_pool(name="sb", bufs=1))
+        ps = ctx.enter_context(tc.psum_pool(name="ps", bufs=1))
+
+        offs_t = sb.tile([P, S // 16], U16, name="offs_t")
+        cell_t = sb.tile([P, S // 16], U16, name="cell_t")
+        xw = [sb.tile([P, T], U32, name=f"xw{o}", align_bytes=64) for o in range(PASSES)]
+        xs = sb.tile([P, T], U8, name="xs", align_bytes=64)
+        wraw = [[sb.tile([P, 4, N], F32, name=f"wraw{o}{h}") for h in range(2)] for o in range(PASSES)]
+        cm = sb.tile([P, U], F32, name="cm")
+        cap_t = sb.tile([P, S], F32, name="cap_t")
+        rate_t = sb.tile([P, 1], F32, name="rate_t")
+        keep_t = sb.tile([P, 1], F32, name="keep_t")
+        ident = sb.tile([P, P], F32, name="ident")
+
+        nc.vector.memset(xs[:].bitcast(I32), 0)
+        one = sb.tile([P, 1], F32, name="one")
+        warm = sb.tile([P, 1], F32, name="warm")
+        nc.gpsimd.memset(one[:], 1.0)
+        nc.scalar.activation(out=warm[:], in_=one[:], func=ACT.Ln, bias=0.1)
+        make_identity(nc, ident[:])
+
+        def load_words(o):
+            nc.sync.dma_start(out=xw[o][:].bitcast(I32), in_=x_words[o].rearrange("p n t -> p (n t)").bitcast(I32))
+
+        def load_w(o):
+            for h, w in enumerate((w1, w2)):
+                nc.sync.dma_start(out=wraw[o][h][:], in_=w[512 * o : 512 * (o + 1), :].rearrange("(p j) n -> p j n", j=4))
+
+        load_words(0)
+        nc.sync.dma_start(offs_t[:], offs)
+        for q in range(4):
+            nc.scalar.dma_start(
+                out=xs[32 * q : 32 * q + 8, :].bitcast(I32), in_=x_scales[:, 4 * q : 4 * q + 4, :].bitcast(I32)
+            )
+        load_w(0)
+        load_words(1)
+        load_w(1)
+        nc.sync.dma_start(cell_t[:], cell)
+        nc.sync.dma_start(out=cm[:], in_=cmap)
+        nc.sync.dma_start(out=cap_t[:], in_=cap)
+        nc.sync.dma_start(out=rate_t[:], in_=rate)
+
+        gw = [sb.tile([P, S], U32, name=f"gw{o}", align_bytes=64) for o in range(PASSES)]
+        gs = sb.tile([P, S], U8, name="gs", align_bytes=64)
+        wbf = [sb.tile([P, 2 * N * 4], BF16, name=f"wbf{o}", align_bytes=64) for o in range(PASSES)]
+        wq = [sb.tile([P, 2 * N], U32, name=f"wq{o}", align_bytes=64) for o in range(PASSES)]
+        wsc = [sb.tile([P, 2 * N], U8, name=f"wsc{o}", align_bytes=64) for o in range(PASSES)]
+
+        def interleave(o):
+            for h in range(2):
+                nc.scalar.copy(
+                    out=wbf[o][:, 4 * N * h : 4 * N * (h + 1)].rearrange("p (c i t) -> p c t i", i=4, t=4),
+                    in_=wraw[o][h][:].rearrange("p t (c i) -> p c t i", i=4),
+                )
+
+        def quantize(o):
+            nc.vector.quantize_mx(out=wq[o][:].bitcast(FP8X4), scales=wsc[o][:], in_=wbf[o][:])
+
+        nc.vector.tensor_copy(gw[0][:], xw[0][:].indirect(offs_t[:]))
+        nc.vector.tensor_copy(gs[:], xs[:].indirect(offs_t[:]))
+        interleave(0)
+        quantize(0)
+        H = S // 2
+        nc.vector.tensor_copy(gw[1][:, :H], xw[1][:].indirect(offs_t[:, : H // 16]))
+        interleave(1)
+        quantize(1)
+        nc.vector.tensor_copy(gw[1][:, H:], xw[1][:].indirect(offs_t[:, H // 16 :]))
+
+        nc.scalar.activation(out=keep_t[:], in_=rate_t[:], func=ACT.Identity, scale=-1.0, bias=1.0)
+        m0 = sb.tile([P, S], F32, name="m0")
+        lim = sb.tile([P, S], F32, name="lim")
+        kept = sb.tile([P, S], F32, name="kept")
+        nc.vector.tensor_copy(m0[:], cm[:].indirect(cell_t[:]))
+        nc.vector.tensor_tensor(lim[:], m0[:], cap_t[:], ALU.add)
+
+        ab = [ps.tile([P, 2 * N], F32, name=f"ab{c}") for c in range(NCH)]
+        pw = [ps.tile([P, CH], F32, name=f"pw{c}") for c in range(NCH)]
+        sq = [sb.tile([P, 2 * N], F32, name=f"sq{c}") for c in range(NCH)]
+        z = [sb.tile([P, CH], F32, name=f"z{c}") for c in range(NCH)]
+        t = [sb.tile([P, CH], F32, name=f"t{c}") for c in range(NCH)]
+
+        def cols(c):
+            return slice(c * CH, (c + 1) * CH)
+
+        def product(c):
+            for o in range(PASSES):
+                nc.tensor.matmul_mx(
+                    out=ab[c][:],
+                    lhsT=gw[o][:, cols(c)].bitcast(FP8X4),
+                    lhsT_scale=gs[4 * o : P, cols(c)],
+                    rhs=wq[o][:].bitcast(FP8X4),
+                    rhs_scale=wsc[o][:],
+                    start=(o == 0),
+                    stop=(o == PASSES - 1),
+                )
+            nc.scalar.activation(out=sq[c][:], in_=ab[c][:], func=ACT.Square)
+
+        def power(c):
+            for h in range(2):
+                nc.tensor.matmul(
+                    out=pw[c][:], lhsT=sq[c][:, h * N : (h + 1) * N], rhs=ident[:],
+                    is_transpose=True, start=(h == 0), stop=(h == 1),
+                )
+            nc.scalar.activation(out=z[c][:], in_=pw[c][:], func=ACT.Ln, bias=0.1)
+            nc.vector.tensor_tensor(t[c][:], z[c][:], lim[:, cols(c)], ALU.min)
+
+        def put(c):
+            v = sq[(c + 1) % NCH][:, :CH]
+            nc.scalar.activation(out=v, in_=t[c][:], func=ACT.Copy, scale=rate_t[:])
+            nc.vector.tensor_tensor(
+                cm[:].indirect(cell_t[:, c * CH // 16 : (c + 1) * CH // 16]), v, kept[:, cols(c)], ALU.add
+            )
+
+        product(0)
+        product(1)
+        power(0)
+        nc.scalar.activation(out=kept[:], in_=m0[:], func=ACT.Copy, scale=keep_t[:])
+        for c in range(NCH):
+            if c + 2 < NCH:
+                product(c + 2)
+            if c + 1 < NCH:
+                power(c + 1)
+            put(c)
+
+        nc.sync.dma_start(out=out, in_=cm[:])

@@ -15,9 +15,14 @@ ALU = mybir.AluOpType
 
 P = 128
 K, T, S, N, U = 1024, 1024, 512, 128, 1024
-PASSES = 2
-CH = 128
-NCH = S // CH
+PACK = 4
+K_PASS = P * PACK
+PASSES = K // K_PASS
+QUADRANT = 32
+GROUP = 16
+CHUNK = 128
+CHUNKS = S // CHUNK
+FLOOR = 0.1
 FLOPS = 2 * 2 * K * N * S
 
 
@@ -29,125 +34,168 @@ def tile_picked_yclut_put_p_kernel(
         sb = ctx.enter_context(tc.tile_pool(name="sb", bufs=1))
         ps = ctx.enter_context(tc.psum_pool(name="ps", bufs=1))
 
-        offs_t = sb.tile([P, S // 16], U16, name="offs_t")
-        cell_t = sb.tile([P, S // 16], U16, name="cell_t")
-        xw = [sb.tile([P, T], U32, name=f"xw{o}", align_bytes=64) for o in range(PASSES)]
-        xs = sb.tile([P, T], U8, name="xs", align_bytes=64)
-        wraw = [[sb.tile([P, 4, N], F32, name=f"wraw{o}{h}") for h in range(2)] for o in range(PASSES)]
-        cm = sb.tile([P, U], F32, name="cm")
+        offs_t = sb.tile([P, S // GROUP], U16, name="offs_t")
+        cell_t = sb.tile([P, S // GROUP], U16, name="cell_t")
+        words = [sb.tile([P, T], U32, name=f"words{o}", align_bytes=64) for o in range(PASSES)]
+        scales = sb.tile([P, T], U8, name="scales", align_bytes=64)
+        w1_raw = sb.tile([P, PASSES, PACK * N], F32, name="w1_raw")
+        w2_raw = [sb.tile([P, PACK * N], F32, name=f"w2_raw{o}") for o in range(PASSES)]
+        cells = sb.tile([P, U], F32, name="cells")
         cap_t = sb.tile([P, S], F32, name="cap_t")
         rate_t = sb.tile([P, 1], F32, name="rate_t")
         keep_t = sb.tile([P, 1], F32, name="keep_t")
         ident = sb.tile([P, P], F32, name="ident")
 
-        nc.vector.memset(xs[:].bitcast(I32), 0)
+        nc.gpsimd.memset(scales[:].bitcast(I32), 0)
         one = sb.tile([P, 1], F32, name="one")
         warm = sb.tile([P, 1], F32, name="warm")
         nc.gpsimd.memset(one[:], 1.0)
-        nc.scalar.activation(out=warm[:], in_=one[:], func=ACT.Ln, bias=0.1)
         make_identity(nc, ident[:])
 
         def load_words(o):
-            nc.sync.dma_start(out=xw[o][:].bitcast(I32), in_=x_words[o].rearrange("p n t -> p (n t)").bitcast(I32))
-
-        def load_w(o):
-            for h, w in enumerate((w1, w2)):
-                nc.sync.dma_start(out=wraw[o][h][:], in_=w[512 * o : 512 * (o + 1), :].rearrange("(p j) n -> p j n", j=4))
+            nc.sync.dma_start(
+                out=words[o][:].bitcast(I32), in_=x_words[o].rearrange("p n t -> p (n t)").bitcast(I32)
+            )
 
         load_words(0)
         nc.sync.dma_start(offs_t[:], offs)
-        for q in range(4):
-            nc.scalar.dma_start(
-                out=xs[32 * q : 32 * q + 8, :].bitcast(I32), in_=x_scales[:, 4 * q : 4 * q + 4, :].bitcast(I32)
+        for q in range(P // QUADRANT):
+            nc.sync.dma_start(
+                out=scales[QUADRANT * q : QUADRANT * q + PASSES * PACK, :].bitcast(I32),
+                in_=x_scales[:, PACK * q : PACK * (q + 1), :].bitcast(I32),
             )
-        load_w(0)
+        nc.scalar.activation(out=warm[:], in_=one[:], func=ACT.Ln, bias=FLOOR)
+        nc.sync.dma_start(out=w1_raw[:], in_=w1.rearrange("(o p j) n -> p o (j n)", o=PASSES, j=PACK))
+        for o in range(PASSES):
+            nc.sync.dma_start(
+                out=w2_raw[o][:], in_=w2[K_PASS * o : K_PASS * (o + 1), :].rearrange("(p j) n -> p (j n)", j=PACK)
+            )
         load_words(1)
-        load_w(1)
+        nc.sync.dma_start(out=cells[:], in_=cmap)
         nc.sync.dma_start(cell_t[:], cell)
-        nc.sync.dma_start(out=cm[:], in_=cmap)
-        nc.sync.dma_start(out=cap_t[:], in_=cap)
         nc.sync.dma_start(out=rate_t[:], in_=rate)
+        nc.sync.dma_start(out=cap_t[:], in_=cap)
 
-        gw = [sb.tile([P, S], U32, name=f"gw{o}", align_bytes=64) for o in range(PASSES)]
-        gs = sb.tile([P, S], U8, name="gs", align_bytes=64)
-        wbf = [sb.tile([P, 2 * N * 4], BF16, name=f"wbf{o}", align_bytes=64) for o in range(PASSES)]
-        wq = [sb.tile([P, 2 * N], U32, name=f"wq{o}", align_bytes=64) for o in range(PASSES)]
-        wsc = [sb.tile([P, 2 * N], U8, name=f"wsc{o}", align_bytes=64) for o in range(PASSES)]
+        picked = [sb.tile([P, S], U32, name=f"picked{o}", align_bytes=64) for o in range(PASSES)]
+        picked_scales = sb.tile([P, S], U8, name="picked_scales", align_bytes=64)
+        w_bf16 = [sb.tile([P, 2 * N * PACK], BF16, name=f"w_bf16_{o}", align_bytes=64) for o in range(PASSES)]
+        w_words = [sb.tile([P, 2 * N], U32, name=f"w_words{o}", align_bytes=64) for o in range(PASSES)]
+        w_scales = [sb.tile([P, 2 * N], U8, name=f"w_scales{o}", align_bytes=64) for o in range(PASSES)]
 
-        def interleave(o):
-            for h in range(2):
-                nc.scalar.copy(
-                    out=wbf[o][:, 4 * N * h : 4 * N * (h + 1)].rearrange("p (c i t) -> p c t i", i=4, t=4),
-                    in_=wraw[o][h][:].rearrange("p t (c i) -> p c t i", i=4),
-                )
+        def interleave(copy, o, h):
+            copy(
+                out=w_bf16[o][:, PACK * N * h : PACK * N * (h + 1)].rearrange("p (c i t) -> p c t i", i=4, t=PACK),
+                in_=(w1_raw[:, o, :], w2_raw[o][:])[h].rearrange("p (t c i) -> p c t i", t=PACK, i=4),
+            )
 
         def quantize(o):
-            nc.vector.quantize_mx(out=wq[o][:].bitcast(FP8X4), scales=wsc[o][:], in_=wbf[o][:])
+            nc.vector.quantize_mx(out=w_words[o][:].bitcast(FP8X4), scales=w_scales[o][:], in_=w_bf16[o][:])
 
-        nc.vector.tensor_copy(gw[0][:], xw[0][:].indirect(offs_t[:]))
-        nc.vector.tensor_copy(gs[:], xs[:].indirect(offs_t[:]))
-        interleave(0)
-        quantize(0)
-        H = S // 2
-        nc.vector.tensor_copy(gw[1][:, :H], xw[1][:].indirect(offs_t[:, : H // 16]))
-        interleave(1)
-        quantize(1)
-        nc.vector.tensor_copy(gw[1][:, H:], xw[1][:].indirect(offs_t[:, H // 16 :]))
-
-        nc.scalar.activation(out=keep_t[:], in_=rate_t[:], func=ACT.Identity, scale=-1.0, bias=1.0)
+        products = [ps.tile([P, 2 * N], F32, name=f"products{c}") for c in range(CHUNKS)]
+        power = [ps.tile([P, CHUNK], F32, name=f"power{c}") for c in range(CHUNKS)]
+        squares = [sb.tile([P, 2 * N], F32, name=f"squares{c}") for c in range(CHUNKS)]
+        z = sb.tile([P, 2 * CHUNK], F32, name="z")
         m0 = sb.tile([P, S], F32, name="m0")
-        lim = sb.tile([P, S], F32, name="lim")
-        kept = sb.tile([P, S], F32, name="kept")
-        nc.vector.tensor_copy(m0[:], cm[:].indirect(cell_t[:]))
-        nc.vector.tensor_tensor(lim[:], m0[:], cap_t[:], ALU.add)
+        limits = sb.tile([P, 2 * CHUNK], F32, name="limits")
+        kept = sb.tile([P, 3 * CHUNK], F32, name="kept")
+        limit_of = {(0, 1): limits[:, :CHUNK], (1, 2): kept[:, :CHUNK], (2, 4): limits[:]}
+        kept_head = squares[0][:, :CHUNK]
+        target = sb.tile([P, S], F32, name="target")
+        step = sb.tile([P, S], F32, name="step")
 
-        ab = [ps.tile([P, 2 * N], F32, name=f"ab{c}") for c in range(NCH)]
-        pw = [ps.tile([P, CH], F32, name=f"pw{c}") for c in range(NCH)]
-        sq = [sb.tile([P, 2 * N], F32, name=f"sq{c}") for c in range(NCH)]
-        z = [sb.tile([P, CH], F32, name=f"z{c}") for c in range(NCH)]
-        t = [sb.tile([P, CH], F32, name=f"t{c}") for c in range(NCH)]
+        def cols(c0, c1):
+            return slice(c0 * CHUNK, c1 * CHUNK)
 
-        def cols(c):
-            return slice(c * CH, (c + 1) * CH)
+        def list_cols(c0, c1):
+            return slice(c0 * CHUNK // GROUP, c1 * CHUNK // GROUP)
 
-        def product(c):
-            for o in range(PASSES):
-                nc.tensor.matmul_mx(
-                    out=ab[c][:],
-                    lhsT=gw[o][:, cols(c)].bitcast(FP8X4),
-                    lhsT_scale=gs[4 * o : P, cols(c)],
-                    rhs=wq[o][:].bitcast(FP8X4),
-                    rhs_scale=wsc[o][:],
-                    start=(o == 0),
-                    stop=(o == PASSES - 1),
-                )
-            nc.scalar.activation(out=sq[c][:], in_=ab[c][:], func=ACT.Square)
-
-        def power(c):
-            for h in range(2):
-                nc.tensor.matmul(
-                    out=pw[c][:], lhsT=sq[c][:, h * N : (h + 1) * N], rhs=ident[:],
-                    is_transpose=True, start=(h == 0), stop=(h == 1),
-                )
-            nc.scalar.activation(out=z[c][:], in_=pw[c][:], func=ACT.Ln, bias=0.1)
-            nc.vector.tensor_tensor(t[c][:], z[c][:], lim[:, cols(c)], ALU.min)
-
-        def put(c):
-            v = sq[(c + 1) % NCH][:, :CH]
-            nc.scalar.activation(out=v, in_=t[c][:], func=ACT.Copy, scale=rate_t[:])
-            nc.vector.tensor_tensor(
-                cm[:].indirect(cell_t[:, c * CH // 16 : (c + 1) * CH // 16]), v, kept[:, cols(c)], ALU.add
+        def product(o, c):
+            nc.tensor.matmul_mx(
+                out=products[c][:],
+                lhsT=picked[o][:, cols(c, c + 1)].bitcast(FP8X4),
+                lhsT_scale=picked_scales[PACK * o : P, cols(c, c + 1)],
+                rhs=w_words[o][:].bitcast(FP8X4),
+                rhs_scale=w_scales[o][:],
+                start=(o == 0),
+                stop=(o == PASSES - 1),
             )
 
-        product(0)
-        product(1)
-        power(0)
-        nc.scalar.activation(out=kept[:], in_=m0[:], func=ACT.Copy, scale=keep_t[:])
-        for c in range(NCH):
-            if c + 2 < NCH:
-                product(c + 2)
-            if c + 1 < NCH:
-                power(c + 1)
-            put(c)
+        def square(c):
+            nc.scalar.activation(out=squares[c][:], in_=products[c][:], func=ACT.Square)
 
-        nc.sync.dma_start(out=out, in_=cm[:])
+        def log_power(c):
+            for h in range(2):
+                nc.tensor.matmul(
+                    out=power[c][:],
+                    lhsT=squares[c][:, h * N : (h + 1) * N],
+                    rhs=ident[:],
+                    is_transpose=True,
+                    start=(h == 0),
+                    stop=(h == 1),
+                )
+            nc.scalar.activation(out=z[:, cols(c % 2, c % 2 + 1)], in_=power[c][:], func=ACT.Ln, bias=FLOOR)
+
+        def limit(c0, c1):
+            nc.vector.tensor_tensor(limit_of[c0, c1], m0[:, cols(c0, c1)], cap_t[:, cols(c0, c1)], ALU.add)
+
+        def clip(c0, c1):
+            z_cols = cols(c0 % 2, c0 % 2 + c1 - c0)
+            nc.vector.tensor_tensor(target[:, cols(c0, c1)], z[:, z_cols], limit_of[c0, c1], ALU.min)
+
+        def keep(c0, c1, dst):
+            nc.scalar.activation(out=dst, in_=m0[:, cols(c0, c1)], func=ACT.Copy, scale=keep_t[:])
+
+        def scale(c0, c1):
+            nc.scalar.activation(
+                out=step[:, cols(c0, c1)], in_=target[:, cols(c0, c1)], func=ACT.Copy, scale=rate_t[:]
+            )
+
+        def put(c0, c1, kept_share):
+            nc.vector.tensor_tensor(
+                cells[:].indirect(cell_t[:, list_cols(c0, c1)]), step[:, cols(c0, c1)], kept_share, ALU.add
+            )
+
+        nc.vector.tensor_copy(picked[0][:], words[0][:].indirect(offs_t[:]))
+        nc.vector.tensor_copy(picked_scales[:], scales[:].indirect(offs_t[:]))
+        interleave(nc.scalar.copy, 0, 0)
+        interleave(nc.scalar.copy, 0, 1)
+        interleave(nc.vector.tensor_copy, 1, 0)
+        interleave(nc.scalar.copy, 1, 1)
+        quantize(0)
+        quantize(1)
+        for c in range(CHUNKS):
+            nc.vector.tensor_copy(picked[1][:, cols(c, c + 1)], words[1][:].indirect(offs_t[:, list_cols(c, c + 1)]))
+        for c in range(CHUNKS):
+            product(0, c)
+        nc.scalar.activation(out=keep_t[:], in_=rate_t[:], func=ACT.Identity, scale=-1.0, bias=1.0)
+        for c0, c1 in ((0, 2), (2, 4)):
+            nc.vector.tensor_copy(m0[:, cols(c0, c1)], cells[:].indirect(cell_t[:, list_cols(c0, c1)]))
+        limit(0, 1)
+        limit(1, 2)
+
+        product(1, 0)
+        square(0)
+        product(1, 1)
+        square(1)
+        log_power(0)
+        clip(0, 1)
+        product(1, 2)
+        square(2)
+        log_power(1)
+        clip(1, 2)
+        limit(2, 4)
+        product(1, 3)
+        square(3)
+        keep(0, 1, kept_head)
+        scale(0, 1)
+        put(0, 1, kept_head)
+        log_power(2)
+        scale(1, 2)
+        log_power(3)
+        clip(2, 4)
+        keep(1, 4, kept[:])
+        put(1, 2, kept[:, :CHUNK])
+        scale(2, 4)
+        put(2, 4, kept[:, CHUNK:])
+
+        nc.sync.dma_start(out=out, in_=cells[:])

from contextlib import ExitStack

import concourse.mybir as mybir
from concourse.masks import make_identity

F32 = mybir.dt.float32
BF16 = mybir.dt.bfloat16
I32 = mybir.dt.int32
U32 = mybir.dt.uint32
U16 = mybir.dt.uint16
U8 = mybir.dt.uint8
FP8X4 = mybir.dt.float8_e4m3fn_x4
ACT = mybir.ActivationFunctionType
ALU = mybir.AluOpType

P = 128
K, T, S, N, U = 1024, 1024, 512, 128, 1024
PACK = 4
K_PASS = P * PACK
PASSES = K // K_PASS
QUADRANT = 32
GROUP = 16
CHUNK = 128
CHUNKS = S // CHUNK
FLOOR = 0.1
FLOPS = 2 * 2 * K * N * S


def tile_picked_yclut_put_p_kernel(
    tc, x_words, x_scales, w1, w2, cmap, cap, rate, offs, cell, out
):
    nc = tc.nc
    with ExitStack() as ctx:
        sb = ctx.enter_context(tc.tile_pool(name="sb", bufs=1))
        ps = ctx.enter_context(tc.psum_pool(name="ps", bufs=1))

        offs_t = sb.tile([P, S // GROUP], U16, name="offs_t")
        cell_t = sb.tile([P, S // GROUP], U16, name="cell_t")
        words = [sb.tile([P, T], U32, name=f"words{o}", align_bytes=64) for o in range(PASSES)]
        scales = sb.tile([P, T], U8, name="scales", align_bytes=64)
        w1_raw = sb.tile([P, PASSES, PACK * N], F32, name="w1_raw")
        w2_raw = [sb.tile([P, PACK * N], F32, name=f"w2_raw{o}") for o in range(PASSES)]
        cells = sb.tile([P, U], F32, name="cells")
        cap_t = sb.tile([P, S], F32, name="cap_t")
        rate_t = sb.tile([P, 1], F32, name="rate_t")
        keep_t = sb.tile([P, 1], F32, name="keep_t")
        ident = sb.tile([P, P], F32, name="ident")

        nc.gpsimd.memset(scales[:].bitcast(I32), 0)
        one = sb.tile([P, 1], F32, name="one")
        warm = sb.tile([P, 1], F32, name="warm")
        nc.gpsimd.memset(one[:], 1.0)
        make_identity(nc, ident[:])

        def load_words(o):
            nc.sync.dma_start(
                out=words[o][:].bitcast(I32), in_=x_words[o].rearrange("p n t -> p (n t)").bitcast(I32)
            )

        load_words(0)
        nc.sync.dma_start(offs_t[:], offs)
        for q in range(P // QUADRANT):
            nc.sync.dma_start(
                out=scales[QUADRANT * q : QUADRANT * q + PASSES * PACK, :].bitcast(I32),
                in_=x_scales[:, PACK * q : PACK * (q + 1), :].bitcast(I32),
            )
        nc.scalar.activation(out=warm[:], in_=one[:], func=ACT.Ln, bias=FLOOR)
        nc.sync.dma_start(out=w1_raw[:], in_=w1.rearrange("(o p j) n -> p o (j n)", o=PASSES, j=PACK))
        for o in range(PASSES):
            nc.sync.dma_start(
                out=w2_raw[o][:], in_=w2[K_PASS * o : K_PASS * (o + 1), :].rearrange("(p j) n -> p (j n)", j=PACK)
            )
        load_words(1)
        nc.sync.dma_start(out=cells[:], in_=cmap)
        nc.sync.dma_start(cell_t[:], cell)
        nc.sync.dma_start(out=rate_t[:], in_=rate)
        nc.sync.dma_start(out=cap_t[:], in_=cap)

        picked = [sb.tile([P, S], U32, name=f"picked{o}", align_bytes=64) for o in range(PASSES)]
        picked_scales = sb.tile([P, S], U8, name="picked_scales", align_bytes=64)
        w_bf16 = [sb.tile([P, 2 * N * PACK], BF16, name=f"w_bf16_{o}", align_bytes=64) for o in range(PASSES)]
        w_words = [sb.tile([P, 2 * N], U32, name=f"w_words{o}", align_bytes=64) for o in range(PASSES)]
        w_scales = [sb.tile([P, 2 * N], U8, name=f"w_scales{o}", align_bytes=64) for o in range(PASSES)]

        def interleave(copy, o, h):
            copy(
                out=w_bf16[o][:, PACK * N * h : PACK * N * (h + 1)].rearrange("p (c i t) -> p c t i", i=4, t=PACK),
                in_=(w1_raw[:, o, :], w2_raw[o][:])[h].rearrange("p (t c i) -> p c t i", t=PACK, i=4),
            )

        def quantize(o):
            nc.vector.quantize_mx(out=w_words[o][:].bitcast(FP8X4), scales=w_scales[o][:], in_=w_bf16[o][:])

        products = [ps.tile([P, 2 * N], F32, name=f"products{c}") for c in range(CHUNKS)]
        power = [ps.tile([P, CHUNK], F32, name=f"power{c}") for c in range(CHUNKS)]
        squares = [sb.tile([P, 2 * N], F32, name=f"squares{c}") for c in range(CHUNKS)]
        z = sb.tile([P, 2 * CHUNK], F32, name="z")
        m0 = sb.tile([P, S], F32, name="m0")
        limits = sb.tile([P, 2 * CHUNK], F32, name="limits")
        kept = sb.tile([P, 3 * CHUNK], F32, name="kept")
        limit_of = {(0, 1): limits[:, :CHUNK], (1, 2): kept[:, :CHUNK], (2, 4): limits[:]}
        kept_head = squares[0][:, :CHUNK]
        target = sb.tile([P, S], F32, name="target")
        step = sb.tile([P, S], F32, name="step")

        def cols(c0, c1):
            return slice(c0 * CHUNK, c1 * CHUNK)

        def list_cols(c0, c1):
            return slice(c0 * CHUNK // GROUP, c1 * CHUNK // GROUP)

        def product(o, c):
            nc.tensor.matmul_mx(
                out=products[c][:],
                lhsT=picked[o][:, cols(c, c + 1)].bitcast(FP8X4),
                lhsT_scale=picked_scales[PACK * o : P, cols(c, c + 1)],
                rhs=w_words[o][:].bitcast(FP8X4),
                rhs_scale=w_scales[o][:],
                start=(o == 0),
                stop=(o == PASSES - 1),
            )

        def square(c):
            nc.scalar.activation(out=squares[c][:], in_=products[c][:], func=ACT.Square)

        def log_power(c):
            for h in range(2):
                nc.tensor.matmul(
                    out=power[c][:],
                    lhsT=squares[c][:, h * N : (h + 1) * N],
                    rhs=ident[:],
                    is_transpose=True,
                    start=(h == 0),
                    stop=(h == 1),
                )
            nc.scalar.activation(out=z[:, cols(c % 2, c % 2 + 1)], in_=power[c][:], func=ACT.Ln, bias=FLOOR)

        def limit(c0, c1):
            nc.vector.tensor_tensor(limit_of[c0, c1], m0[:, cols(c0, c1)], cap_t[:, cols(c0, c1)], ALU.add)

        def clip(c0, c1):
            z_cols = cols(c0 % 2, c0 % 2 + c1 - c0)
            nc.vector.tensor_tensor(target[:, cols(c0, c1)], z[:, z_cols], limit_of[c0, c1], ALU.min)

        def keep(c0, c1, dst):
            nc.scalar.activation(out=dst, in_=m0[:, cols(c0, c1)], func=ACT.Copy, scale=keep_t[:])

        def scale(c0, c1):
            nc.scalar.activation(
                out=step[:, cols(c0, c1)], in_=target[:, cols(c0, c1)], func=ACT.Copy, scale=rate_t[:]
            )

        def put(c0, c1, kept_share):
            nc.vector.tensor_tensor(
                cells[:].indirect(cell_t[:, list_cols(c0, c1)]), step[:, cols(c0, c1)], kept_share, ALU.add
            )

        nc.vector.tensor_copy(picked[0][:], words[0][:].indirect(offs_t[:]))
        nc.vector.tensor_copy(picked_scales[:], scales[:].indirect(offs_t[:]))
        interleave(nc.scalar.copy, 0, 0)
        interleave(nc.scalar.copy, 0, 1)
        interleave(nc.vector.tensor_copy, 1, 0)
        interleave(nc.scalar.copy, 1, 1)
        quantize(0)
        quantize(1)
        for c in range(CHUNKS):
            nc.vector.tensor_copy(picked[1][:, cols(c, c + 1)], words[1][:].indirect(offs_t[:, list_cols(c, c + 1)]))
        for c in range(CHUNKS):
            product(0, c)
        nc.scalar.activation(out=keep_t[:], in_=rate_t[:], func=ACT.Identity, scale=-1.0, bias=1.0)
        for c0, c1 in ((0, 2), (2, 4)):
            nc.vector.tensor_copy(m0[:, cols(c0, c1)], cells[:].indirect(cell_t[:, list_cols(c0, c1)]))
        limit(0, 1)
        limit(1, 2)

        product(1, 0)
        square(0)
        product(1, 1)
        square(1)
        log_power(0)
        clip(0, 1)
        product(1, 2)
        square(2)
        log_power(1)
        clip(1, 2)
        limit(2, 4)
        product(1, 3)
        square(3)
        keep(0, 1, kept_head)
        scale(0, 1)
        put(0, 1, kept_head)
        log_power(2)
        scale(1, 2)
        log_power(3)
        clip(2, 4)
        keep(1, 4, kept[:])
        put(1, 2, kept[:, :CHUNK])
        scale(2, 4)
        put(2, 4, kept[:, CHUNK:])

        nc.sync.dma_start(out=out, in_=cells[:])
